import numpy as np
import ml_dtypes


def mxq(x, axis, fmt="e4m3"):
    dtype, down = {"e4m3": (ml_dtypes.float8_e4m3fn, 7), "e5m2": (ml_dtypes.float8_e5m2, 14)}[fmt]
    v = np.moveaxis(np.asarray(x, np.float32).astype(ml_dtypes.bfloat16).astype(np.float64), axis, -1)
    blocks = v.reshape(v.shape[:-1] + (-1, 32))
    amax = np.abs(blocks).max(-1, keepdims=True)
    byte = np.maximum(np.where(amax > 0, np.frexp(amax)[1] - 1 + 127, 0) - down, 1)
    scale = np.exp2(byte - 127.0)
    codes = (blocks / scale).astype(np.float32).astype(dtype).astype(np.float64)
    return np.moveaxis((codes * scale).reshape(v.shape), -1, axis)


WIDE = False


def mx_kscale(k):
    if not WIDE:
        return np.ones(k)
    levels = np.array([10, -10, 5, -5, 0])
    if k % 512:
        return np.exp2(np.random.permutation(np.resize(levels, k // 32))).repeat(32)
    a = np.empty((k // 512, 16))
    for p in range(k // 512):
        a[p, :8] = np.random.permutation(np.resize(levels, 8))
        for g in range(8):
            far = levels[np.abs(levels - a[p, g]) >= 10]
            a[p, g + 8] = far[np.random.randint(len(far))]
    return np.exp2(a.ravel()).repeat(32)


def f64(x):
    return np.asarray(x).astype(np.float64)


def striped(idx):
    return np.tile(np.asarray(idx).reshape(-1, 16).T, (8, 1)).astype(np.uint16)


def unstriped(offs):
    return offs[:16].T.reshape(-1).astype(np.int64)


E2M1 = np.array([0.0, 0.5, 1.0, 1.5, 2.0, 3.0, 4.0, 6.0, -0.0, -0.5, -1.0, -1.5, -2.0, -3.0, -4.0, -6.0])


def pack_weight(w, fmt):
    k, n = w.shape
    w = f64(np.asarray(w, np.float32).astype(ml_dtypes.bfloat16)).reshape(k // 32, 32, n)
    amax = np.abs(w).max(1)
    if fmt == "e4m3":
        byte = np.frexp(amax)[1] - 1 + 127 - 7
    else:
        mant, ex = np.frexp(amax / 6.0)
        byte = np.where(mant > 0.5, ex, ex - 1) + 127
    byte = np.clip(np.where(amax > 0, byte, 1), 1, 254)
    scaled = (w * np.exp2(127.0 - byte)[:, None, :]).reshape(k, n).astype(np.float32)
    by_word = np.ascontiguousarray(scaled.reshape(k // 512, 128, 4, n).transpose(0, 1, 3, 2))
    if fmt == "e4m3":
        words = by_word.astype(ml_dtypes.float8_e4m3fn).view(np.uint8)
    else:
        c = by_word.astype(ml_dtypes.float4_e2m1fn).view(np.uint8) & 0xF
        words = (c[..., 0::2] | (c[..., 1::2] << 4)).reshape(k // 512, 128, 2 * n)
    return np.ascontiguousarray(words), np.ascontiguousarray(byte.astype(np.uint8).reshape(k // 512, 16, n))


def unpack_weight(words, scales, fmt):
    g, _, n = scales.shape
    words = np.ascontiguousarray(words).reshape(g, 128, n, -1)
    if fmt == "e4m3":
        vals = words.view(ml_dtypes.float8_e4m3fn).astype(np.float64)
    else:
        nib = np.empty((g, 128, n, 4), np.uint8)
        nib[..., 0::2] = words & 0xF
        nib[..., 1::2] = words >> 4
        vals = E2M1[nib]
    vals = vals * np.repeat(np.exp2(scales.astype(np.float64) - 127.0), 8, axis=1)[..., None]
    return vals.transpose(0, 1, 3, 2).reshape(g * 512, n)


def sigmoid(v):
    return 1.0 / (1.0 + np.exp(-v))


D, E, T, I, Q = 512, 512, 2048, 512, 128


def setup_inputs():
    n = np.random.standard_normal
    idx = np.random.permutation(T)[:I]
    fd = mx_kscale(D)
    fi = mx_kscale(I)
    ti = np.ones(T)
    ti[idx] = fi
    keysp = pack_weight(n((D, T)) / fd[:, None], "e2m1")
    return {
        "query": (n((D, Q)) * 0.8 / np.sqrt(D) * fd[:, None]).astype(np.float32),
        "keys_words": keysp[0],
        "keys_scales": keysp[1],
        "th": (np.random.uniform(0.4, 1.0, (Q, 1))).astype(np.float32),
        "dquery": (n((D, Q)) * 0.6 / np.sqrt(D) * fd[:, None]).astype(np.float32),
        "os": (np.random.uniform(4.0, 16.0, (1, I)) * fi).astype(np.float32),
        "vals": (n((E, T)) / ti).astype(np.float32),
        "offs": striped(idx),
    }


def reference(query, keys_words, keys_scales, th, dquery, os, vals, offs):
    idx = unstriped(offs)
    keysu = unpack_weight(keys_words, keys_scales, "e2m1")
    queryq = mxq(f64(query), 0, "e4m3")
    keysidxg = keysu[:, idx]
    a = queryq.T @ keysidxg
    dqueryq = mxq(f64(dquery), 0, "e4m3")
    ta = dqueryq.T @ keysidxg
    e1s = sigmoid((f64(th) - np.mean(np.square(a), axis=1, keepdims=True)) * 4.0)
    p = np.exp(a - np.max(a, axis=1, keepdims=True))
    z = np.sum(p, axis=1, keepdims=True)
    te1s = np.mean(ta * a * 2.0, axis=1, keepdims=True) * (-1.0) * 4.0 * e1s * (1.0 - e1s)
    tp = ta * p
    tz = np.sum(tp, axis=1, keepdims=True)
    tw = (tp - tz * p / z) / z * (1.0 - e1s) + te1s * (-1.0) * p / z + te1s / 512.0
    wo1 = tw * f64(os)
    wt1 = wo1.T
    vt1 = f64(vals)[:, idx].T
    wt1q = mxq(wt1, 0, "e4m3")
    vt1q = mxq(vt1, 0, "e4m3")
    o = wt1q.T @ vt1q
    return o

@@ -1,0 +1,213 @@
+from contextlib import ExitStack
+
+import concourse.mybir as mybir
+from concourse.masks import make_identity
+
+D, E, T, I, Q = 512, 512, 2048, 512, 128
+FLOPS = 2 * Q * I * D * 2 + 2 * Q * I * E
+
+F32 = mybir.dt.float32
+BF16 = mybir.dt.bfloat16
+I32 = mybir.dt.int32
+U32 = mybir.dt.uint32
+U16 = mybir.dt.uint16
+U8 = mybir.dt.uint8
+FP8X4 = mybir.dt.float8_e4m3fn_x4
+FP4X4 = mybir.dt.float4_e2m1fn_x4
+ALU = mybir.AluOpType
+ACT = mybir.ActivationFunctionType
+
+P = 128
+PACK = 4
+BLOCKS = E // P
+
+
+def tile_attend_ttevenbyspread_kernel(tc, query, keys_words, keys_scales, th, dquery, slot_factor, vals, offs, out):
+    nc = tc.nc
+    with ExitStack() as ctx:
+        sb = ctx.enter_context(tc.tile_pool(name="sb", bufs=1))
+        ps = ctx.enter_context(tc.psum_pool(name="ps", bufs=1))
+        turn = ctx.enter_context(tc.psum_pool(name="turn", bufs=3))
+
+        def column(name):
+            return sb.tile([P, 1], F32, name=name)
+
+        def mx_tiles(name, tag=None):
+            codes = sb.tile([P, P], U32, name=name + "_codes", tag=tag or name + "_codes", align_bytes=64)
+            scales = sb.tile([P, P], U8, name=name + "_scales", align_bytes=64)
+            return codes[:], scales[:]
+
+        def quantise(operand, grouped):
+            codes, scales = operand
+            nc.vector.quantize_mx(out=codes.bitcast(FP8X4), scales=scales, in_=grouped[:])
+
+        offsets = sb.tile([P, I // 16], U16, name="offsets")
+        nc.sync.dma_start(offsets[:], offs)
+
+        def load_rows(name, src):
+            rows = sb.tile([P, PACK, Q], F32, name=name)
+            nc.sync.dma_start(rows[:], src.rearrange("(p t) q -> p t q", t=PACK))
+            return rows
+
+        raw = [load_rows("query_rows", query)]
+        key_pool = sb.tile([P, T], U16, name="key_pool")
+        nc.sync.dma_start(key_pool[:].bitcast(I32), keys_words[0].bitcast(I32))
+        scale_pool = sb.tile([P, T], U8, name="scale_pool")
+        nc.vector.memset(scale_pool[:].bitcast(I32), 0)
+        for quad in range(4):
+            nc.scalar.dma_start(
+                scale_pool[32 * quad : 32 * quad + 4, :].bitcast(I32),
+                keys_scales[0, 4 * quad : 4 * quad + 4, :].bitcast(I32),
+            )
+        raw.append(load_rows("dquery_rows", dquery))
+        val_pool = []
+        for b in range(BLOCKS):
+            rows = sb.tile([P, T], F32, name="val_pool%d" % b, align_bytes=64)
+            nc.sync.dma_start(rows[:], vals[b * P : (b + 1) * P, :])
+            val_pool.append(rows)
+        th_col = column("th_col")
+        nc.gpsimd.dma_start(th_col[:], th)
+        os_cols = sb.tile([P, PACK], F32, name="os_cols")
+        nc.gpsimd.dma_start(os_cols[:], slot_factor.rearrange("o (p t) -> p (o t)", t=PACK))
+        ident = sb.tile([P, P], F32, name="ident")
+        make_identity(nc, ident[:])
+        th2 = column("th2")
+        nc.gpsimd.tensor_scalar(th2[:], th_col[:], 2.0, 0.0, ALU.mult, ALU.add)
+
+        key_scales = sb.tile([P, I], U8, name="key_scales", align_bytes=64)
+        nc.vector.tensor_copy(key_scales[:], scale_pool[:].indirect(offsets[:]))
+        key_words = sb.tile([P, I], U16, name="key_words", align_bytes=64)
+        nc.vector.tensor_copy(key_words[:], key_pool[:].indirect(offsets[:]))
+        scores = []
+        for name, rows in zip(("a", "ta"), raw):
+            grouped = sb.tile([P, Q * PACK], BF16, name=name + "_grouped", align_bytes=64)
+            nc.scalar.copy(
+                grouped[:].rearrange("p (c i t) -> p c t i", i=4, t=PACK),
+                rows[:].rearrange("p t (c i) -> p c t i", i=4),
+            )
+            operand = mx_tiles(name)
+            quantise(operand, grouped)
+            bank = ps.tile([P, I], F32, name=name + "_bank")
+            nc.tensor.matmul_mx(
+                out=bank[:],
+                lhsT=operand[0].bitcast(FP8X4),
+                lhsT_scale=operand[1],
+                rhs=key_words[:].bitcast(FP4X4),
+                rhs_scale=key_scales[:],
+                start=True,
+                stop=True,
+            )
+            scores.append(bank[:].rearrange("q (s t) -> q t s", t=PACK))
+        a_dealt, ta_dealt = scores
+
+        def dealt(name):
+            return sb.tile([P, PACK, P], F32, name=name, align_bytes=64)
+
+        neg_a, prob, ta_p = dealt("neg_a"), dealt("prob"), dealt("ta_p")
+        neg_max, z, sum_sq, cross, tz = (column(n) for n in ("neg_max", "z", "sum_sq", "cross", "tz"))
+        nc.vector.tensor_scalar(neg_a[:], a_dealt, -1.0, None, ALU.mult, ALU.min, accum_out=neg_max[:])
+        nc.scalar.activation(prob[:], neg_a[:], ACT.Exp, bias=neg_max[:], scale=-1.0, accum_out=z[:])
+        a_sq, ta_a = dealt("a_sq"), dealt("ta_a")
+        nc.scalar.activation(a_sq[:], neg_a[:], ACT.Square, accum_out=sum_sq[:])
+        nc.vector.scalar_tensor_tensor(
+            ta_a[:], ta_dealt, -4.0 / I, neg_a[:], ALU.mult, ALU.mult, accum_out=cross[:]
+        )
+        rz, neg_rz, cross_z = column("rz"), column("neg_rz"), column("cross_z")
+        nc.vector.reciprocal(rz[:], z[:])
+        nc.vector.tensor_scalar(cross_z[:], cross[:], z[:], -1.0 / I, ALU.mult, ALU.mult)
+        nc.vector.scalar_tensor_tensor(
+            ta_p[:], ta_dealt, 1.0, prob[:], ALU.mult, ALU.mult, accum_out=tz[:]
+        )
+        nc.vector.tensor_scalar(neg_rz[:], rz[:], -1.0, None, ALU.mult)
+
+        h, shift0, c1 = column("h"), column("shift0"), column("c1")
+        pre = sb.tile([P, 2], F32, name="pre")
+        c23 = sb.tile([P, 2], F32, name="c23", align_bytes=64)
+        nc.scalar.activation(h[:], sum_sq[:], ACT.Tanh, bias=th2[:], scale=-2.0 / I)
+        nc.scalar.activation(shift0[:], tz[:], ACT.Identity, bias=cross[:], scale=neg_rz[:])
+        nc.scalar.activation(c1[:], h[:], ACT.Identity, bias=rz[:], scale=neg_rz[:])
+        nc.scalar.activation(pre[:, 1:2], h[:], ACT.Identity, bias=cross_z[:], scale=cross_z[:])
+        nc.scalar.activation(pre[:, 0:1], h[:], ACT.Identity, bias=shift0[:], scale=cross[:])
+        term_a, term_b = dealt("term_a"), dealt("term_b")
+        nc.scalar.activation(term_a[:], ta_p[:], ACT.Copy, scale=c1[:])
+        nc.scalar.activation(c23[:], pre[:], ACT.Copy, scale=c1[:])
+        nc.scalar.activation(term_b[:], prob[:], ACT.Identity, bias=c23[:, 1:2], scale=c23[:, 0:1])
+
+        def gather_values(b, listed_tag=None, grouped_tag=None):
+            listed = sb.tile(
+                [P, I], BF16, name="listed%d" % b, tag=listed_tag or "listed%d" % b, align_bytes=64
+            )
+            nc.vector.tensor_copy(listed[:], val_pool[b][:].indirect(offsets[:]))
+            words = listed[:].bitcast(F32)
+            bank = turn.tile([P, 2, P], F32, name="turned")
+            for u in range(2):
+                nc.tensor.transpose(bank[:, u, :], words[:, u : I // 2 : 2], ident[:])
+            packed = sb.tile(
+                [P, P * PACK], BF16, name="val_grouped%d" % b, tag=grouped_tag or "val_grouped%d" % b, align_bytes=64
+            )
+            nc.scalar.copy(
+                packed[:].bitcast(F32).rearrange("p (e u) -> p e u", u=2),
+                bank[:].rearrange("p u e -> p e u"),
+            )
+            return packed
+
+        grouped = [gather_values(0, "neg_a", "prob"), gather_values(1, "a_sq", "c23")]
+
+        w_bank = ps.tile([P, PACK, Q], F32, name="w_bank")
+        for n, term in enumerate((term_a, term_b)):
+            for t in range(PACK):
+                nc.tensor.matmul(
+                    w_bank[:, t, :],
+                    term[:, t, :],
+                    ident[:],
+                    start=(n == 0 and t == 0),
+                    stop=(n == 1 and t == PACK - 1),
+                    is_transpose=True,
+                )
+        grouped.append(gather_values(2))
+        w_grouped = sb.tile([P, Q * PACK], BF16, name="w_grouped", tag="val_pool2", align_bytes=64)
+        nc.vector.scalar_tensor_tensor(
+            w_grouped[:].rearrange("p (q t) -> p q t", t=PACK),
+            w_bank[:].rearrange("p t q -> p q t"),
+            0.5,
+            os_cols[:].unsqueeze(1).to_broadcast([P, Q, PACK]),
+            ALU.mult,
+            ALU.mult,
+        )
+        grouped.append(gather_values(3))
+
+        late_codes = sb.tile([P, BLOCKS * P], U32, name="late_codes", tag="val_pool3", align_bytes=64)
+        late_scales = sb.tile([P, BLOCKS * P], U8, name="late_scales", align_bytes=64)
+        late = [(late_codes[:, n * P : (n + 1) * P], late_scales[:, n * P : (n + 1) * P]) for n in range(BLOCKS)]
+        w_mx = late[0]
+        val_mx = late[1:]
+        quantise(w_mx, w_grouped)
+        for b in range(BLOCKS - 1):
+            quantise(val_mx[b], grouped[b])
+
+        def product(bank, b):
+            nc.tensor.matmul_mx(
+                out=bank,
+                lhsT=w_mx[0].bitcast(FP8X4),
+                lhsT_scale=w_mx[1],
+                rhs=val_mx[b][0].bitcast(FP8X4),
+                rhs_scale=val_mx[b][1],
+                start=True,
+                stop=True,
+            )
+
+        early = (BLOCKS - 1) * P
+        early_bank = ps.tile([P, early], F32, name="early_bank")
+        for b in range(BLOCKS - 1):
+            product(early_bank[:, b * P : (b + 1) * P], b)
+        early_out = sb.tile([P, early], F32, name="early_out")
+        nc.scalar.copy(early_out[:], early_bank[:])
+        nc.sync.dma_start(out[:, :early], early_out[:])
+
+        val_mx.append(mx_tiles("val3"))
+        quantise(val_mx[3], grouped[3])
+        last_bank = ps.tile([P, P], F32, name="last_bank")
+        product(last_bank[:], 3)
+        last_out = sb.tile([P, P], F32, name="last_out")
+        nc.vector.tensor_copy(last_out[:], last_bank[:])
+        nc.sync.dma_start(out[:, early:], last_out[:])

@@ -20,6 +20,7 @@ ACT = mybir.ActivationFunctionType
 P = 128
 PACK = 4
 BLOCKS = E // P
+HALF = I // 2
 
 
 def tile_attend_ttevenbyspread_kernel(tc, query, keys_words, keys_scales, th, dquery, slot_factor, vals, offs, out):
@@ -27,13 +28,13 @@ def tile_attend_ttevenbyspread_kernel(tc, query, keys_words, keys_scales, th, dq
     with ExitStack() as ctx:
         sb = ctx.enter_context(tc.tile_pool(name="sb", bufs=1))
         ps = ctx.enter_context(tc.psum_pool(name="ps", bufs=1))
-        turn = ctx.enter_context(tc.psum_pool(name="turn", bufs=3))
 
-        def column(name):
-            return sb.tile([P, 1], F32, name=name)
+        def column(name, tag=None):
+            return sb.tile([P, 1], F32, name=name, tag=tag or name, align_bytes=64)
 
-        def mx_tiles(name, tag=None):
-            codes = sb.tile([P, P], U32, name=name + "_codes", tag=tag or name + "_codes", align_bytes=64)
+        def mx_tiles(name, codes=None):
+            if codes is None:
+                codes = sb.tile([P, P], U32, name=name + "_codes", align_bytes=64)
             scales = sb.tile([P, P], U8, name=name + "_scales", align_bytes=64)
             return codes[:], scales[:]
 
@@ -41,25 +42,22 @@ def tile_attend_ttevenbyspread_kernel(tc, query, keys_words, keys_scales, th, dq
             codes, scales = operand
             nc.vector.quantize_mx(out=codes.bitcast(FP8X4), scales=scales, in_=grouped[:])
 
+        scale_pool = sb.tile([P, T], U8, name="scale_pool", align_bytes=64)
+        nc.vector.memset(scale_pool[:].bitcast(I32), 0)
         offsets = sb.tile([P, I // 16], U16, name="offsets")
         nc.sync.dma_start(offsets[:], offs)
-
-        def load_rows(name, src):
-            rows = sb.tile([P, PACK, Q], F32, name=name)
-            nc.sync.dma_start(rows[:], src.rearrange("(p t) q -> p t q", t=PACK))
-            return rows
-
-        raw = [load_rows("query_rows", query)]
         key_pool = sb.tile([P, T], U16, name="key_pool")
         nc.sync.dma_start(key_pool[:].bitcast(I32), keys_words[0].bitcast(I32))
-        scale_pool = sb.tile([P, T], U8, name="scale_pool")
-        nc.vector.memset(scale_pool[:].bitcast(I32), 0)
         for quad in range(4):
             nc.scalar.dma_start(
                 scale_pool[32 * quad : 32 * quad + 4, :].bitcast(I32),
                 keys_scales[0, 4 * quad : 4 * quad + 4, :].bitcast(I32),
             )
-        raw.append(load_rows("dquery_rows", dquery))
+        raw = []
+        for name, src in (("query_rows", query), ("dquery_rows", dquery)):
+            rows = sb.tile([P, PACK, Q], F32, name=name, align_bytes=64)
+            nc.sync.dma_start(rows[:], src.rearrange("(p t) q -> p t q", t=PACK))
+            raw.append(rows)
         val_pool = []
         for b in range(BLOCKS):
             rows = sb.tile([P, T], F32, name="val_pool%d" % b, align_bytes=64)
@@ -74,85 +72,110 @@ def tile_attend_ttevenbyspread_kernel(tc, query, keys_words, keys_scales, th, dq
         th2 = column("th2")
         nc.gpsimd.tensor_scalar(th2[:], th_col[:], 2.0, 0.0, ALU.mult, ALU.add)
 
-        key_scales = sb.tile([P, I], U8, name="key_scales", align_bytes=64)
-        nc.vector.tensor_copy(key_scales[:], scale_pool[:].indirect(offsets[:]))
-        key_words = sb.tile([P, I], U16, name="key_words", align_bytes=64)
-        nc.vector.tensor_copy(key_words[:], key_pool[:].indirect(offsets[:]))
-        scores = []
-        for name, rows in zip(("a", "ta"), raw):
-            grouped = sb.tile([P, Q * PACK], BF16, name=name + "_grouped", align_bytes=64)
+        def quantise_rows(name, rows, grouped, codes=None):
             nc.scalar.copy(
                 grouped[:].rearrange("p (c i t) -> p c t i", i=4, t=PACK),
                 rows[:].rearrange("p t (c i) -> p c t i", i=4),
             )
-            operand = mx_tiles(name)
+            operand = mx_tiles(name, codes)
             quantise(operand, grouped)
-            bank = ps.tile([P, I], F32, name=name + "_bank")
+            return operand
+
+        key_words = sb.tile([P, I], U16, name="key_words", align_bytes=64)
+        nc.vector.tensor_copy(key_words[:], key_pool[:].indirect(offsets[:]))
+
+        def score(bank, operand, slots):
             nc.tensor.matmul_mx(
-                out=bank[:],
+                out=bank,
                 lhsT=operand[0].bitcast(FP8X4),
                 lhsT_scale=operand[1],
-                rhs=key_words[:].bitcast(FP4X4),
-                rhs_scale=key_scales[:],
+                rhs=key_words[:, slots].bitcast(FP4X4),
+                rhs_scale=key_scales[:, slots],
                 start=True,
                 stop=True,
             )
-            scores.append(bank[:].rearrange("q (s t) -> q t s", t=PACK))
-        a_dealt, ta_dealt = scores
+
+        query_grouped = sb.tile([P, Q * PACK], BF16, name="query_grouped", align_bytes=64)
+        query_mx = quantise_rows("query", raw[0], query_grouped)
+        key_scales = sb.tile([P, I], U8, name="key_scales", tag="query_rows", align_bytes=64)
+        a_banks = []
+        for n in range(2):
+            slots = slice(n * HALF, (n + 1) * HALF)
+            nc.vector.tensor_copy(
+                key_scales[:, slots], scale_pool[:].indirect(offsets[:, n * HALF // 16 : (n + 1) * HALF // 16])
+            )
+            a_bank = ps.tile([P, HALF], F32, name="a_bank%d" % n, tag="shared_bank", bufs=2)
+            a_banks.append(a_bank)
+            score(a_bank[:], query_mx, slots)
+        dquery_codes = sb.tile([P, P], U32, name="dquery_codes", tag="scale_pool", align_bytes=64)
+        dquery_grouped = sb.tile([P, Q * PACK], BF16, name="dquery_grouped", align_bytes=64)
+        dquery_mx = quantise_rows("dquery", raw[1], dquery_grouped, dquery_codes)
+        ta_bank = ps.tile([P, I], F32, name="ta_bank")
+        score(ta_bank[:], dquery_mx, slice(0, I))
+        def gather(b, tag):
+            listed = sb.tile([P, I], BF16, name="listed%d" % b, tag=tag, align_bytes=64)
+            nc.vector.tensor_copy(listed[:], val_pool[b][:].indirect(offsets[:]))
+            return listed
+
+        def turn(b, listed, bank_tag):
+            words = listed[:].bitcast(F32)
+            bank = ps.tile([P, 2, P], F32, name="turned%d" % b, tag=bank_tag)
+            for u in range(2):
+                nc.tensor.transpose(bank[:, u, :], words[:, u : I // 2 : 2], ident[:])
+            return bank
+
+        def group_values(grouped, bank):
+            nc.scalar.copy(
+                grouped.bitcast(F32).rearrange("p (e u) -> p e u", u=2), bank[:].rearrange("p u e -> p e u")
+            )
 
         def dealt(name):
             return sb.tile([P, PACK, P], F32, name=name, align_bytes=64)
 
-        neg_a, prob, ta_p = dealt("neg_a"), dealt("prob"), dealt("ta_p")
-        neg_max, z, sum_sq, cross, tz = (column(n) for n in ("neg_max", "z", "sum_sq", "cross", "tz"))
-        nc.vector.tensor_scalar(neg_a[:], a_dealt, -1.0, None, ALU.mult, ALU.min, accum_out=neg_max[:])
-        nc.scalar.activation(prob[:], neg_a[:], ACT.Exp, bias=neg_max[:], scale=-1.0, accum_out=z[:])
-        a_sq, ta_a = dealt("a_sq"), dealt("ta_a")
+        neg_a, prob = dealt("neg_a"), dealt("prob")
+        neg_max = None
+        for n in range(2):
+            so_far = neg_max
+            neg_max = column("neg_max%d" % n)[:]
+            nc.vector.tensor_scalar(
+                neg_a[:, :, n * HALF // PACK : (n + 1) * HALF // PACK],
+                a_banks[n][:].rearrange("q (s t) -> q t s", t=PACK),
+                -1.0,
+                so_far,
+                ALU.mult,
+                ALU.min,
+                accum_out=neg_max,
+            )
+        ta_dealt = ta_bank[:].rearrange("q (s t) -> q t s", t=PACK)
+        z, sum_sq = column("z"), column("sum_sq")
+        nc.scalar.activation(prob[:], neg_a[:], ACT.Exp, bias=neg_max, scale=-1.0, accum_out=z[:])
+        a_sq = dealt("a_sq")
         nc.scalar.activation(a_sq[:], neg_a[:], ACT.Square, accum_out=sum_sq[:])
+        turned0 = turn(0, gather(0, "query_scales"), "turned01")
+        rz, neg_rz = column("rz"), column("neg_rz")
+        nc.vector.reciprocal(rz[:], z[:])
+        nc.gpsimd.tensor_scalar(neg_rz[:], rz[:], -1.0, 0.0, ALU.mult, ALU.add)
+        ta_a, cross = dealt("ta_a"), column("cross", "neg_max1")
         nc.vector.scalar_tensor_tensor(
             ta_a[:], ta_dealt, -4.0 / I, neg_a[:], ALU.mult, ALU.mult, accum_out=cross[:]
         )
-        rz, neg_rz, cross_z = column("rz"), column("neg_rz"), column("cross_z")
-        nc.vector.reciprocal(rz[:], z[:])
-        nc.vector.tensor_scalar(cross_z[:], cross[:], z[:], -1.0 / I, ALU.mult, ALU.mult)
-        nc.vector.scalar_tensor_tensor(
-            ta_p[:], ta_dealt, 1.0, prob[:], ALU.mult, ALU.mult, accum_out=tz[:]
+        h, c1, even, g, c1_g, c1_tz, c2, c3 = (
+            column(n) for n in ("h", "c1", "even", "g", "c1_g", "c1_tz", "c2", "c3")
         )
-        nc.vector.tensor_scalar(neg_rz[:], rz[:], -1.0, None, ALU.mult)
-
-        h, shift0, c1 = column("h"), column("shift0"), column("c1")
-        pre = sb.tile([P, 2], F32, name="pre")
-        c23 = sb.tile([P, 2], F32, name="c23", align_bytes=64)
         nc.scalar.activation(h[:], sum_sq[:], ACT.Tanh, bias=th2[:], scale=-2.0 / I)
-        nc.scalar.activation(shift0[:], tz[:], ACT.Identity, bias=cross[:], scale=neg_rz[:])
         nc.scalar.activation(c1[:], h[:], ACT.Identity, bias=rz[:], scale=neg_rz[:])
-        nc.scalar.activation(pre[:, 1:2], h[:], ACT.Identity, bias=cross_z[:], scale=cross_z[:])
-        nc.scalar.activation(pre[:, 0:1], h[:], ACT.Identity, bias=shift0[:], scale=cross[:])
         term_a, term_b = dealt("term_a"), dealt("term_b")
-        nc.scalar.activation(term_a[:], ta_p[:], ACT.Copy, scale=c1[:])
-        nc.scalar.activation(c23[:], pre[:], ACT.Copy, scale=c1[:])
-        nc.scalar.activation(term_b[:], prob[:], ACT.Identity, bias=c23[:, 1:2], scale=c23[:, 0:1])
+        nc.vector.scalar_tensor_tensor(
+            term_a[:], ta_dealt, c1[:], prob[:], ALU.mult, ALU.mult, accum_out=c1_tz[:]
+        )
+        nc.scalar.activation(even[:], h[:], ACT.Copy, bias=-1.0 / I, scale=1.0 / I)
+        nc.scalar.activation(g[:], h[:], ACT.Identity, bias=cross[:], scale=cross[:])
+        nc.scalar.activation(c1_g[:], g[:], ACT.Copy, scale=c1[:])
+        nc.scalar.activation(c3[:], g[:], ACT.Copy, scale=even[:])
+        nc.scalar.activation(c2[:], c1_tz[:], ACT.Identity, bias=c1_g[:], scale=neg_rz[:])
+        nc.scalar.activation(term_b[:], prob[:], ACT.Identity, bias=c3[:], scale=c2[:])
 
-        def gather_values(b, listed_tag=None, grouped_tag=None):
-            listed = sb.tile(
-                [P, I], BF16, name="listed%d" % b, tag=listed_tag or "listed%d" % b, align_bytes=64
-            )
-            nc.vector.tensor_copy(listed[:], val_pool[b][:].indirect(offsets[:]))
-            words = listed[:].bitcast(F32)
-            bank = turn.tile([P, 2, P], F32, name="turned")
-            for u in range(2):
-                nc.tensor.transpose(bank[:, u, :], words[:, u : I // 2 : 2], ident[:])
-            packed = sb.tile(
-                [P, P * PACK], BF16, name="val_grouped%d" % b, tag=grouped_tag or "val_grouped%d" % b, align_bytes=64
-            )
-            nc.scalar.copy(
-                packed[:].bitcast(F32).rearrange("p (e u) -> p e u", u=2),
-                bank[:].rearrange("p u e -> p e u"),
-            )
-            return packed
-
-        grouped = [gather_values(0, "neg_a", "prob"), gather_values(1, "a_sq", "c23")]
-
+        width = P * PACK
         w_bank = ps.tile([P, PACK, Q], F32, name="w_bank")
         for n, term in enumerate((term_a, term_b)):
             for t in range(PACK):
@@ -164,8 +187,11 @@ def tile_attend_ttevenbyspread_kernel(tc, query, keys_words, keys_scales, th, dq
                     stop=(n == 1 and t == PACK - 1),
                     is_transpose=True,
                 )
-        grouped.append(gather_values(2))
-        w_grouped = sb.tile([P, Q * PACK], BF16, name="w_grouped", tag="val_pool2", align_bytes=64)
+        pair = sb.tile([P, 2 * width], BF16, name="pair", tag="prob", align_bytes=64)
+        group_values(pair[:, :width], turned0)
+        group_values(pair[:, width:], turn(1, gather(1, "rz"), "turned01"))
+        listed2 = gather(2, "h")
+        w_grouped = sb.tile([P, width], BF16, name="w_grouped", align_bytes=64)
         nc.vector.scalar_tensor_tensor(
             w_grouped[:].rearrange("p (q t) -> p q t", t=PACK),
             w_bank[:].rearrange("p t q -> p q t"),
@@ -174,40 +200,39 @@ def tile_attend_ttevenbyspread_kernel(tc, query, keys_words, keys_scales, th, dq
             ALU.mult,
             ALU.mult,
         )
-        grouped.append(gather_values(3))
+        third = sb.tile([P, width], BF16, name="third", align_bytes=64)
+        group_values(third[:], turn(2, listed2, "w_bank"))
+        last_grouped = sb.tile([P, width], BF16, name="last_grouped", align_bytes=64)
+        group_values(last_grouped[:], turn(3, gather(3, "term_b"), "turned3"))
 
-        late_codes = sb.tile([P, BLOCKS * P], U32, name="late_codes", tag="val_pool3", align_bytes=64)
-        late_scales = sb.tile([P, BLOCKS * P], U8, name="late_scales", align_bytes=64)
-        late = [(late_codes[:, n * P : (n + 1) * P], late_scales[:, n * P : (n + 1) * P]) for n in range(BLOCKS)]
-        w_mx = late[0]
-        val_mx = late[1:]
-        quantise(w_mx, w_grouped)
-        for b in range(BLOCKS - 1):
-            quantise(val_mx[b], grouped[b])
+        front_codes = sb.tile([P, BLOCKS * P], U32, name="front_codes", tag="val_pool3", align_bytes=64)
+        front_scales = sb.tile([P, BLOCKS * P], U8, name="front_scales", align_bytes=64)
+        for lo, hi, grouped in ((P, 3 * P, pair), (0, P, w_grouped), (3 * P, 4 * P, third)):
+            quantise((front_codes[:, lo:hi], front_scales[:, lo:hi]), grouped)
+        last_mx = mx_tiles("last")
+        quantise(last_mx, last_grouped)
 
-        def product(bank, b):
+        def product(bank, codes, scales):
             nc.tensor.matmul_mx(
                 out=bank,
-                lhsT=w_mx[0].bitcast(FP8X4),
-                lhsT_scale=w_mx[1],
-                rhs=val_mx[b][0].bitcast(FP8X4),
-                rhs_scale=val_mx[b][1],
+                lhsT=front_codes[:, :P].bitcast(FP8X4),
+                lhsT_scale=front_scales[:, :P],
+                rhs=codes.bitcast(FP8X4),
+                rhs_scale=scales,
                 start=True,
                 stop=True,
             )
 
         early = (BLOCKS - 1) * P
-        early_bank = ps.tile([P, early], F32, name="early_bank")
-        for b in range(BLOCKS - 1):
-            product(early_bank[:, b * P : (b + 1) * P], b)
+        early_bank = ps.tile([P, early], F32, name="early_bank", tag="shared_bank", bufs=2)
+        for lo, hi in ((0, 2 * P), (2 * P, early)):
+            product(early_bank[:, lo:hi], front_codes[:, P + lo : P + hi], front_scales[:, P + lo : P + hi])
         early_out = sb.tile([P, early], F32, name="early_out")
         nc.scalar.copy(early_out[:], early_bank[:])
         nc.sync.dma_start(out[:, :early], early_out[:])
 
-        val_mx.append(mx_tiles("val3"))
-        quantise(val_mx[3], grouped[3])
-        last_bank = ps.tile([P, P], F32, name="last_bank")
-        product(last_bank[:], 3)
+        last_bank = ps.tile([P, P], F32, name="last_bank", tag="shared_bank", bufs=2)
+        product(last_bank[:], last_mx[0], last_mx[1])
         last_out = sb.tile([P, P], F32, name="last_out")
         nc.vector.tensor_copy(last_out[:], last_bank[:])
         nc.sync.dma_start(out[:, early:], last_out[:])

@@ -98,15 +98,13 @@ def tile_attend_ttevenbyspread_kernel(tc, query, keys_words, keys_scales, th, dq
         query_grouped = sb.tile([P, Q * PACK], BF16, name="query_grouped", align_bytes=64)
         query_mx = quantise_rows("query", raw[0], query_grouped)
         key_scales = sb.tile([P, I], U8, name="key_scales", tag="query_rows", align_bytes=64)
-        a_banks = []
+        a_bank = ps.tile([P, I], F32, name="a_bank")
         for n in range(2):
             slots = slice(n * HALF, (n + 1) * HALF)
             nc.vector.tensor_copy(
                 key_scales[:, slots], scale_pool[:].indirect(offsets[:, n * HALF // 16 : (n + 1) * HALF // 16])
             )
-            a_bank = ps.tile([P, HALF], F32, name="a_bank%d" % n, tag="shared_bank", bufs=2)
-            a_banks.append(a_bank)
-            score(a_bank[:], query_mx, slots)
+            score(a_bank[:, slots], query_mx, slots)
         dquery_codes = sb.tile([P, P], U32, name="dquery_codes", tag="scale_pool", align_bytes=64)
         dquery_grouped = sb.tile([P, Q * PACK], BF16, name="dquery_grouped", align_bytes=64)
         dquery_mx = quantise_rows("dquery", raw[1], dquery_grouped, dquery_codes)
@@ -133,29 +131,26 @@ def tile_attend_ttevenbyspread_kernel(tc, query, keys_words, keys_scales, th, dq
             return sb.tile([P, PACK, P], F32, name=name, align_bytes=64)
 
         neg_a, prob = dealt("neg_a"), dealt("prob")
-        neg_max = None
-        for n in range(2):
-            so_far = neg_max
-            neg_max = column("neg_max%d" % n)[:]
-            nc.vector.tensor_scalar(
-                neg_a[:, :, n * HALF // PACK : (n + 1) * HALF // PACK],
-                a_banks[n][:].rearrange("q (s t) -> q t s", t=PACK),
-                -1.0,
-                so_far,
-                ALU.mult,
-                ALU.min,
-                accum_out=neg_max,
-            )
+        neg_max = column("neg_max")
+        nc.vector.tensor_scalar(
+            neg_a[:],
+            a_bank[:].rearrange("q (s t) -> q t s", t=PACK),
+            -1.0,
+            None,
+            ALU.mult,
+            ALU.min,
+            accum_out=neg_max[:],
+        )
         ta_dealt = ta_bank[:].rearrange("q (s t) -> q t s", t=PACK)
         z, sum_sq = column("z"), column("sum_sq")
-        nc.scalar.activation(prob[:], neg_a[:], ACT.Exp, bias=neg_max, scale=-1.0, accum_out=z[:])
+        nc.scalar.activation(prob[:], neg_a[:], ACT.Exp, bias=neg_max[:], scale=-1.0, accum_out=z[:])
         a_sq = dealt("a_sq")
         nc.scalar.activation(a_sq[:], neg_a[:], ACT.Square, accum_out=sum_sq[:])
         turned0 = turn(0, gather(0, "query_scales"), "turned01")
         rz, neg_rz = column("rz"), column("neg_rz")
         nc.vector.reciprocal(rz[:], z[:])
         nc.gpsimd.tensor_scalar(neg_rz[:], rz[:], -1.0, 0.0, ALU.mult, ALU.add)
-        ta_a, cross = dealt("ta_a"), column("cross", "neg_max1")
+        ta_a, cross = dealt("ta_a"), column("cross", "neg_max")
         nc.vector.scalar_tensor_tensor(
             ta_a[:], ta_dealt, -4.0 / I, neg_a[:], ALU.mult, ALU.mult, accum_out=cross[:]
         )
@@ -224,14 +219,14 @@ def tile_attend_ttevenbyspread_kernel(tc, query, keys_words, keys_scales, th, dq
             )
 
         early = (BLOCKS - 1) * P
-        early_bank = ps.tile([P, early], F32, name="early_bank", tag="shared_bank", bufs=2)
+        early_bank = ps.tile([P, early], F32, name="early_bank")
         for lo, hi in ((0, 2 * P), (2 * P, early)):
             product(early_bank[:, lo:hi], front_codes[:, P + lo : P + hi], front_scales[:, P + lo : P + hi])
         early_out = sb.tile([P, early], F32, name="early_out")
         nc.scalar.copy(early_out[:], early_bank[:])
         nc.sync.dma_start(out[:, :early], early_out[:])
 
-        last_bank = ps.tile([P, P], F32, name="last_bank", tag="shared_bank", bufs=2)
+        last_bank = ps.tile([P, P], F32, name="last_bank")
         product(last_bank[:], last_mx[0], last_mx[1])
         last_out = sb.tile([P, P], F32, name="last_out")
         nc.vector.tensor_copy(last_out[:], last_bank[:])

@@ -202,14 +202,16 @@ def tile_attend_ttevenbyspread_kernel(tc, query, keys_words, keys_scales, th, dq
 
         front_codes = sb.tile([P, BLOCKS * P], U32, name="front_codes", tag="val_pool3", align_bytes=64)
         front_scales = sb.tile([P, BLOCKS * P], U8, name="front_scales", align_bytes=64)
-        for lo, hi, grouped in ((P, 3 * P, pair), (0, P, w_grouped), (3 * P, 4 * P, third)):
+        for lo, hi, grouped in ((0, P, w_grouped), (P, 3 * P, pair), (3 * P, 4 * P, third)):
             quantise((front_codes[:, lo:hi], front_scales[:, lo:hi]), grouped)
         last_mx = mx_tiles("last")
         quantise(last_mx, last_grouped)
 
-        def product(bank, codes, scales):
+        def finish(name, first, codes, scales, copy):
+            count = scales.shape[1]
+            bank = ps.tile([P, count], F32, name=name + "_bank")
             nc.tensor.matmul_mx(
-                out=bank,
+                out=bank[:],
                 lhsT=front_codes[:, :P].bitcast(FP8X4),
                 lhsT_scale=front_scales[:, :P],
                 rhs=codes.bitcast(FP8X4),
@@ -217,17 +219,10 @@ def tile_attend_ttevenbyspread_kernel(tc, query, keys_words, keys_scales, th, dq
                 start=True,
                 stop=True,
             )
+            result = sb.tile([P, count], F32, name=name + "_out")
+            copy(result[:], bank[:])
+            nc.sync.dma_start(out[:, first : first + count], result[:])
 
-        early = (BLOCKS - 1) * P
-        early_bank = ps.tile([P, early], F32, name="early_bank")
-        for lo, hi in ((0, 2 * P), (2 * P, early)):
-            product(early_bank[:, lo:hi], front_codes[:, P + lo : P + hi], front_scales[:, P + lo : P + hi])
-        early_out = sb.tile([P, early], F32, name="early_out")
-        nc.scalar.copy(early_out[:], early_bank[:])
-        nc.sync.dma_start(out[:, :early], early_out[:])
-
-        last_bank = ps.tile([P, P], F32, name="last_bank")
-        product(last_bank[:], last_mx[0], last_mx[1])
-        last_out = sb.tile([P, P], F32, name="last_out")
-        nc.vector.tensor_copy(last_out[:], last_bank[:])
-        nc.sync.dma_start(out[:, early:], last_out[:])
+        finish("pair", 0, front_codes[:, P : 3 * P], front_scales[:, P : 3 * P], nc.scalar.copy)
+        finish("third", 2 * P, front_codes[:, 3 * P :], front_scales[:, 3 * P :], nc.scalar.copy)
+        finish("last", 3 * P, last_mx[0], last_mx[1], nc.vector.tensor_copy)

from contextlib import ExitStack

import concourse.mybir as mybir
from concourse.masks import make_identity

D, E, T, I, Q = 512, 512, 2048, 512, 128
FLOPS = 2 * Q * I * D * 2 + 2 * Q * I * E

F32 = mybir.dt.float32
BF16 = mybir.dt.bfloat16
I32 = mybir.dt.int32
U32 = mybir.dt.uint32
U16 = mybir.dt.uint16
U8 = mybir.dt.uint8
FP8X4 = mybir.dt.float8_e4m3fn_x4
FP4X4 = mybir.dt.float4_e2m1fn_x4
ALU = mybir.AluOpType
ACT = mybir.ActivationFunctionType

P = 128
PACK = 4
BLOCKS = E // P
HALF = I // 2


def tile_attend_ttevenbyspread_kernel(tc, query, keys_words, keys_scales, th, dquery, slot_factor, vals, offs, out):
    nc = tc.nc
    with ExitStack() as ctx:
        sb = ctx.enter_context(tc.tile_pool(name="sb", bufs=1))
        ps = ctx.enter_context(tc.psum_pool(name="ps", bufs=1))

        def column(name, tag=None):
            return sb.tile([P, 1], F32, name=name, tag=tag or name, align_bytes=64)

        def mx_tiles(name, codes=None):
            if codes is None:
                codes = sb.tile([P, P], U32, name=name + "_codes", align_bytes=64)
            scales = sb.tile([P, P], U8, name=name + "_scales", align_bytes=64)
            return codes[:], scales[:]

        def quantise(operand, grouped):
            codes, scales = operand
            nc.vector.quantize_mx(out=codes.bitcast(FP8X4), scales=scales, in_=grouped[:])

        scale_pool = sb.tile([P, T], U8, name="scale_pool", align_bytes=64)
        nc.vector.memset(scale_pool[:].bitcast(I32), 0)
        offsets = sb.tile([P, I // 16], U16, name="offsets")
        nc.sync.dma_start(offsets[:], offs)
        key_pool = sb.tile([P, T], U16, name="key_pool")
        nc.sync.dma_start(key_pool[:].bitcast(I32), keys_words[0].bitcast(I32))
        for quad in range(4):
            nc.scalar.dma_start(
                scale_pool[32 * quad : 32 * quad + 4, :].bitcast(I32),
                keys_scales[0, 4 * quad : 4 * quad + 4, :].bitcast(I32),
            )
        raw = []
        for name, src in (("query_rows", query), ("dquery_rows", dquery)):
            rows = sb.tile([P, PACK, Q], F32, name=name, align_bytes=64)
            nc.sync.dma_start(rows[:], src.rearrange("(p t) q -> p t q", t=PACK))
            raw.append(rows)
        val_pool = []
        for b in range(BLOCKS):
            rows = sb.tile([P, T], F32, name="val_pool%d" % b, align_bytes=64)
            nc.sync.dma_start(rows[:], vals[b * P : (b + 1) * P, :])
            val_pool.append(rows)
        th_col = column("th_col")
        nc.gpsimd.dma_start(th_col[:], th)
        os_cols = sb.tile([P, PACK], F32, name="os_cols")
        nc.gpsimd.dma_start(os_cols[:], slot_factor.rearrange("o (p t) -> p (o t)", t=PACK))
        ident = sb.tile([P, P], F32, name="ident")
        make_identity(nc, ident[:])
        th2 = column("th2")
        nc.gpsimd.tensor_scalar(th2[:], th_col[:], 2.0, 0.0, ALU.mult, ALU.add)

        def quantise_rows(name, rows, grouped, codes=None):
            nc.scalar.copy(
                grouped[:].rearrange("p (c i t) -> p c t i", i=4, t=PACK),
                rows[:].rearrange("p t (c i) -> p c t i", i=4),
            )
            operand = mx_tiles(name, codes)
            quantise(operand, grouped)
            return operand

        key_words = sb.tile([P, I], U16, name="key_words", align_bytes=64)
        nc.vector.tensor_copy(key_words[:], key_pool[:].indirect(offsets[:]))

        def score(bank, operand, slots):
            nc.tensor.matmul_mx(
                out=bank,
                lhsT=operand[0].bitcast(FP8X4),
                lhsT_scale=operand[1],
                rhs=key_words[:, slots].bitcast(FP4X4),
                rhs_scale=key_scales[:, slots],
                start=True,
                stop=True,
            )

        query_grouped = sb.tile([P, Q * PACK], BF16, name="query_grouped", align_bytes=64)
        query_mx = quantise_rows("query", raw[0], query_grouped)
        key_scales = sb.tile([P, I], U8, name="key_scales", tag="query_rows", align_bytes=64)
        a_bank = ps.tile([P, I], F32, name="a_bank")
        for n in range(2):
            slots = slice(n * HALF, (n + 1) * HALF)
            nc.vector.tensor_copy(
                key_scales[:, slots], scale_pool[:].indirect(offsets[:, n * HALF // 16 : (n + 1) * HALF // 16])
            )
            score(a_bank[:, slots], query_mx, slots)
        dquery_codes = sb.tile([P, P], U32, name="dquery_codes", tag="scale_pool", align_bytes=64)
        dquery_grouped = sb.tile([P, Q * PACK], BF16, name="dquery_grouped", align_bytes=64)
        dquery_mx = quantise_rows("dquery", raw[1], dquery_grouped, dquery_codes)
        ta_bank = ps.tile([P, I], F32, name="ta_bank")
        score(ta_bank[:], dquery_mx, slice(0, I))
        def gather(b, tag):
            listed = sb.tile([P, I], BF16, name="listed%d" % b, tag=tag, align_bytes=64)
            nc.vector.tensor_copy(listed[:], val_pool[b][:].indirect(offsets[:]))
            return listed

        def turn(b, listed, bank_tag):
            words = listed[:].bitcast(F32)
            bank = ps.tile([P, 2, P], F32, name="turned%d" % b, tag=bank_tag)
            for u in range(2):
                nc.tensor.transpose(bank[:, u, :], words[:, u : I // 2 : 2], ident[:])
            return bank

        def group_values(grouped, bank):
            nc.scalar.copy(
                grouped.bitcast(F32).rearrange("p (e u) -> p e u", u=2), bank[:].rearrange("p u e -> p e u")
            )

        def dealt(name):
            return sb.tile([P, PACK, P], F32, name=name, align_bytes=64)

        neg_a, prob = dealt("neg_a"), dealt("prob")
        neg_max = column("neg_max")
        nc.vector.tensor_scalar(
            neg_a[:],
            a_bank[:].rearrange("q (s t) -> q t s", t=PACK),
            -1.0,
            None,
            ALU.mult,
            ALU.min,
            accum_out=neg_max[:],
        )
        ta_dealt = ta_bank[:].rearrange("q (s t) -> q t s", t=PACK)
        z, sum_sq = column("z"), column("sum_sq")
        nc.scalar.activation(prob[:], neg_a[:], ACT.Exp, bias=neg_max[:], scale=-1.0, accum_out=z[:])
        a_sq = dealt("a_sq")
        nc.scalar.activation(a_sq[:], neg_a[:], ACT.Square, accum_out=sum_sq[:])
        turned0 = turn(0, gather(0, "query_scales"), "turned01")
        rz, neg_rz = column("rz"), column("neg_rz")
        nc.vector.reciprocal(rz[:], z[:])
        nc.gpsimd.tensor_scalar(neg_rz[:], rz[:], -1.0, 0.0, ALU.mult, ALU.add)
        ta_a, cross = dealt("ta_a"), column("cross", "neg_max")
        nc.vector.scalar_tensor_tensor(
            ta_a[:], ta_dealt, -4.0 / I, neg_a[:], ALU.mult, ALU.mult, accum_out=cross[:]
        )
        h, c1, even, g, c1_g, c1_tz, c2, c3 = (
            column(n) for n in ("h", "c1", "even", "g", "c1_g", "c1_tz", "c2", "c3")
        )
        nc.scalar.activation(h[:], sum_sq[:], ACT.Tanh, bias=th2[:], scale=-2.0 / I)
        nc.scalar.activation(c1[:], h[:], ACT.Identity, bias=rz[:], scale=neg_rz[:])
        term_a, term_b = dealt("term_a"), dealt("term_b")
        nc.vector.scalar_tensor_tensor(
            term_a[:], ta_dealt, c1[:], prob[:], ALU.mult, ALU.mult, accum_out=c1_tz[:]
        )
        nc.scalar.activation(even[:], h[:], ACT.Copy, bias=-1.0 / I, scale=1.0 / I)
        nc.scalar.activation(g[:], h[:], ACT.Identity, bias=cross[:], scale=cross[:])
        nc.scalar.activation(c1_g[:], g[:], ACT.Copy, scale=c1[:])
        nc.scalar.activation(c3[:], g[:], ACT.Copy, scale=even[:])
        nc.scalar.activation(c2[:], c1_tz[:], ACT.Identity, bias=c1_g[:], scale=neg_rz[:])
        nc.scalar.activation(term_b[:], prob[:], ACT.Identity, bias=c3[:], scale=c2[:])

        width = P * PACK
        w_bank = ps.tile([P, PACK, Q], F32, name="w_bank")
        for n, term in enumerate((term_a, term_b)):
            for t in range(PACK):
                nc.tensor.matmul(
                    w_bank[:, t, :],
                    term[:, t, :],
                    ident[:],
                    start=(n == 0 and t == 0),
                    stop=(n == 1 and t == PACK - 1),
                    is_transpose=True,
                )
        pair = sb.tile([P, 2 * width], BF16, name="pair", tag="prob", align_bytes=64)
        group_values(pair[:, :width], turned0)
        group_values(pair[:, width:], turn(1, gather(1, "rz"), "turned01"))
        listed2 = gather(2, "h")
        w_grouped = sb.tile([P, width], BF16, name="w_grouped", align_bytes=64)
        nc.vector.scalar_tensor_tensor(
            w_grouped[:].rearrange("p (q t) -> p q t", t=PACK),
            w_bank[:].rearrange("p t q -> p q t"),
            0.5,
            os_cols[:].unsqueeze(1).to_broadcast([P, Q, PACK]),
            ALU.mult,
            ALU.mult,
        )
        third = sb.tile([P, width], BF16, name="third", align_bytes=64)
        group_values(third[:], turn(2, listed2, "w_bank"))
        last_grouped = sb.tile([P, width], BF16, name="last_grouped", align_bytes=64)
        group_values(last_grouped[:], turn(3, gather(3, "term_b"), "turned3"))

        front_codes = sb.tile([P, BLOCKS * P], U32, name="front_codes", tag="val_pool3", align_bytes=64)
        front_scales = sb.tile([P, BLOCKS * P], U8, name="front_scales", align_bytes=64)
        for lo, hi, grouped in ((0, P, w_grouped), (P, 3 * P, pair), (3 * P, 4 * P, third)):
            quantise((front_codes[:, lo:hi], front_scales[:, lo:hi]), grouped)
        last_mx = mx_tiles("last")
        quantise(last_mx, last_grouped)

        def finish(name, first, codes, scales, copy):
            count = scales.shape[1]
            bank = ps.tile([P, count], F32, name=name + "_bank")
            nc.tensor.matmul_mx(
                out=bank[:],
                lhsT=front_codes[:, :P].bitcast(FP8X4),
                lhsT_scale=front_scales[:, :P],
                rhs=codes.bitcast(FP8X4),
                rhs_scale=scales,
                start=True,
                stop=True,
            )
            result = sb.tile([P, count], F32, name=name + "_out")
            copy(result[:], bank[:])
            nc.sync.dma_start(out[:, first : first + count], result[:])

        finish("pair", 0, front_codes[:, P : 3 * P], front_scales[:, P : 3 * P], nc.scalar.copy)
        finish("third", 2 * P, front_codes[:, 3 * P :], front_scales[:, 3 * P :], nc.scalar.copy)
        finish("last", 3 * P, last_mx[0], last_mx[1], nc.vector.tensor_copy)
